import numpy as np
import ml_dtypes


def mxq(x, axis, fmt="e4m3"):
    dtype, down = {"e4m3": (ml_dtypes.float8_e4m3fn, 7), "e5m2": (ml_dtypes.float8_e5m2, 14)}[fmt]
    v = np.moveaxis(np.asarray(x, np.float32).astype(ml_dtypes.bfloat16).astype(np.float64), axis, -1)
    blocks = v.reshape(v.shape[:-1] + (-1, 32))
    amax = np.abs(blocks).max(-1, keepdims=True)
    byte = np.maximum(np.where(amax > 0, np.frexp(amax)[1] - 1 + 127, 0) - down, 1)
    scale = np.exp2(byte - 127.0)
    codes = (blocks / scale).astype(np.float32).astype(dtype).astype(np.float64)
    return np.moveaxis((codes * scale).reshape(v.shape), -1, axis)


WIDE = False


def mx_kscale(k):
    if not WIDE:
        return np.ones(k)
    levels = np.array([10, -10, 5, -5, 0])
    if k % 512:
        return np.exp2(np.random.permutation(np.resize(levels, k // 32))).repeat(32)
    a = np.empty((k // 512, 16))
    for p in range(k // 512):
        a[p, :8] = np.random.permutation(np.resize(levels, 8))
        for g in range(8):
            far = levels[np.abs(levels - a[p, g]) >= 10]
            a[p, g + 8] = far[np.random.randint(len(far))]
    return np.exp2(a.ravel()).repeat(32)


def f64(x):
    return np.asarray(x).astype(np.float64)


def striped(idx):
    return np.tile(np.asarray(idx).reshape(-1, 16).T, (8, 1)).astype(np.uint16)


def unstriped(offs):
    return offs[:16].T.reshape(-1).astype(np.int64)


E2M1 = np.array([0.0, 0.5, 1.0, 1.5, 2.0, 3.0, 4.0, 6.0, -0.0, -0.5, -1.0, -1.5, -2.0, -3.0, -4.0, -6.0])


def pack_weight(w, fmt):
    k, n = w.shape
    w = f64(np.asarray(w, np.float32).astype(ml_dtypes.bfloat16)).reshape(k // 32, 32, n)
    amax = np.abs(w).max(1)
    if fmt == "e4m3":
        byte = np.frexp(amax)[1] - 1 + 127 - 7
    else:
        mant, ex = np.frexp(amax / 6.0)
        byte = np.where(mant > 0.5, ex, ex - 1) + 127
    byte = np.clip(np.where(amax > 0, byte, 1), 1, 254)
    scaled = (w * np.exp2(127.0 - byte)[:, None, :]).reshape(k, n).astype(np.float32)
    by_word = np.ascontiguousarray(scaled.reshape(k // 512, 128, 4, n).transpose(0, 1, 3, 2))
    if fmt == "e4m3":
        words = by_word.astype(ml_dtypes.float8_e4m3fn).view(np.uint8)
    else:
        c = by_word.astype(ml_dtypes.float4_e2m1fn).view(np.uint8) & 0xF
        words = (c[..., 0::2] | (c[..., 1::2] << 4)).reshape(k // 512, 128, 2 * n)
    return np.ascontiguousarray(words), np.ascontiguousarray(byte.astype(np.uint8).reshape(k // 512, 16, n))


def unpack_weight(words, scales, fmt):
    g, _, n = scales.shape
    words = np.ascontiguousarray(words).reshape(g, 128, n, -1)
    if fmt == "e4m3":
        vals = words.view(ml_dtypes.float8_e4m3fn).astype(np.float64)
    else:
        nib = np.empty((g, 128, n, 4), np.uint8)
        nib[..., 0::2] = words & 0xF
        nib[..., 1::2] = words >> 4
        vals = E2M1[nib]
    vals = vals * np.repeat(np.exp2(scales.astype(np.float64) - 127.0), 8, axis=1)[..., None]
    return vals.transpose(0, 1, 3, 2).reshape(g * 512, n)


def sigmoid(v):
    return 1.0 / (1.0 + np.exp(-v))


D, E, T, I, Q, G = 512, 512, 2048, 512, 128, 32


def setup_inputs():
    n = np.random.standard_normal
    idx = np.random.permutation(T)[:I]
    fd = mx_kscale(D)
    fe = mx_kscale(E)
    keysp = pack_weight(n((D, T)) / fd[:, None], "e2m1")
    valsp = pack_weight(n((E, T)) / fe[:, None], "e2m1")
    return {
        "query": (n((D, Q)) * 0.7 / np.sqrt(D) * fd[:, None]).astype(np.float32),
        "keys_words": keysp[0],
        "keys_scales": keysp[1],
        "th": (np.random.uniform(-0.2, 0.2, (Q, 1))).astype(np.float32),
        "steep": (np.random.uniform(2.0, 8.0, (Q, 1))).astype(np.float32),
        "gout": (n((E, Q)) * 1 / np.sqrt(E) * fe[:, None]).astype(np.float32),
        "vals_words": valsp[0],
        "vals_scales": valsp[1],
        "size": (np.random.uniform(0.5, 2.0, (1, I))).astype(np.float32),
        "base": (0.5 * n((Q, T))).astype(np.float32),
        "gq1": (np.random.uniform(0.3, 1.5, (Q, 1))).astype(np.float32),
        "offs": striped(idx),
    }


def reference(query, keys_words, keys_scales, th, steep, gout, vals_words, vals_scales, size, base, gq1, offs):
    idx = unstriped(offs)
    keysu = unpack_weight(keys_words, keys_scales, "e2m1")
    valsu = unpack_weight(vals_words, vals_scales, "e2m1")
    queryq = mxq(f64(query), 0, "e4m3")
    keysidxg = keysu[:, idx]
    a = queryq.T @ keysidxg
    s = a.reshape(Q, G, I // G).mean(axis=2)
    gt = sigmoid((s - f64(th)) * f64(steep))
    gr = np.repeat(gt, I // G, axis=1)
    r = np.exp(a - np.max(a, axis=1, keepdims=True))
    p = r * gr
    z = np.sum(p, axis=1, keepdims=True)
    goutq = mxq(f64(gout), 0, "e4m3")
    valsidxg = valsu[:, idx]
    c0 = goutq.T @ valsidxg
    dz = np.sum(c0 * p * f64(size) / np.square(z) * (-1.0), axis=1, keepdims=True)
    dp = c0 / z * f64(size) + dz
    dr = dp * gr
    dgr = dp * r
    dgt = dgr.reshape(Q, G, I // G).sum(axis=2)
    ds = dgt * gt * (1.0 - gt) * f64(steep)
    e1 = ds / 16.0
    r1 = np.repeat(e1, I // G, axis=1)
    da = dr * r + r1
    hda = da * 512.0 * 2.0 * 512.0
    he1 = hda.reshape(Q, G, I // G).sum(axis=2)
    hds = he1 / 16.0
    hdgt = hds * f64(steep) * (1.0 - gt) * gt
    r51 = np.repeat(hdgt, I // G, axis=1)
    hdr = hda * r
    hdp = r51 * r + hdr * gr
    hdz = np.sum(hdp, axis=1, keepdims=True)
    hz = np.sum(hdp * f64(size) * c0 / np.square(z) * (-1.0), axis=1, keepdims=True) + np.sum(hdz * (-1.0) * c0 * p * f64(size) / np.square(np.square(z)) * (-1.0), axis=1, keepdims=True) * z * 2.0
    hp = hdz * (-1.0) / np.square(z) * c0 * f64(size) + hz
    hr = hda * dr + r51 * dp + hp * gr
    hgr = hdr * dp + hp * r
    hgt = hds * f64(steep) * (1.0 - gt) * dgt + hgr.reshape(Q, G, I // G).sum(axis=2) - hds * f64(steep) * dgt * gt
    hs = hgt * gt * (1.0 - gt) * f64(steep)
    e52 = hs / 16.0
    r52 = np.repeat(e52, I // G, axis=1)
    ha = hr * r + r52
    gs = ha * f64(gq1)
    gf = np.zeros((Q, T))
    gf[:, idx] = gs
    y = f64(base) + gf
    return y

@@ -1,0 +1,254 @@
+from contextlib import ExitStack
+
+import concourse.mybir as mybir
+from concourse.masks import make_identity
+
+D, E, T, I, Q, G = 512, 512, 2048, 512, 128, 32
+PAGE = I // G
+P = 128
+PACK = 4
+FLOPS = 2 * 2 * 512 * I * Q
+PENALTY = 512.0 * 2.0 * 512.0
+STORES = 4
+
+F32 = mybir.dt.float32
+BF16 = mybir.dt.bfloat16
+I32 = mybir.dt.int32
+U32 = mybir.dt.uint32
+U16 = mybir.dt.uint16
+U8 = mybir.dt.uint8
+FP8X4 = mybir.dt.float8_e4m3fn_x4
+FP4X4 = mybir.dt.float4_e2m1fn_x4
+ALU = mybir.AluOpType
+ACT = mybir.ActivationFunctionType
+AX = mybir.AxisListType
+
+
+def tile_attend_gppagegate_kernel(
+    tc, query, keys_words, keys_scales, th, steep, gout, vals_words, vals_scales, size, base, gq1, offs, out
+):
+    nc = tc.nc
+    with ExitStack() as ctx:
+        sb = ctx.enter_context(tc.tile_pool(name="sb", bufs=1))
+        ps = ctx.enter_context(tc.psum_pool(name="ps", bufs=1))
+
+        def tile(name, shape, dtype=F32, tag=None):
+            return sb.tile(shape, dtype, name=name, tag=tag or name, align_bytes=64)
+
+        def paged(ap):
+            return ap.rearrange("p (g s) -> p g s", s=PAGE)
+
+        def spread(ap):
+            return ap.unsqueeze(2).to_broadcast([P, G, PAGE])
+
+        offsets = sb.tile([P, I // 16], U16, name="offsets")
+        k_words = tile("k_words", [P, T], U16, tag="pool_a")
+        k_bytes = tile("k_bytes", [P, T], U8)
+        v_words = tile("v_words", [P, T], U16, tag="pool_v")
+        g_raw = tile("g_raw", [P, PACK, Q], tag="raw_g")
+        v_bytes = tile("v_bytes", [P, T], U8)
+        q_raw = tile("q_raw", [P, PACK, Q], tag="raw_q")
+        placed = tile("placed", [P, T])
+        steep_sb = tile("steep_sb", [P, 1])
+        th_sb = tile("th_sb", [P, 1])
+        gq1_sb = tile("gq1_sb", [P, 1])
+        size_sb = tile("size_sb", [P, I // P])
+        warm = tile("warm", [P, 1])
+        warm_out = tile("warm_out", [P, 1])
+
+        nc.vector.memset(k_bytes[:].bitcast(I32), 0)
+        nc.vector.memset(v_bytes[:].bitcast(I32), 0)
+        nc.vector.memset(warm[:], 0.0)
+        nc.vector.memset(placed[:], 0.0)
+        nc.scalar.activation(warm_out[:], warm[:], ACT.Exp)
+
+        def load_bytes(plane, scales):
+            for quad in range(4):
+                nc.sync.dma_start(
+                    out=plane[32 * quad : 32 * quad + 4, :].bitcast(I32),
+                    in_=scales[0, 4 * quad : 4 * quad + 4, :].bitcast(I32),
+                )
+
+        nc.sync.dma_start(offsets[:], offs)
+        nc.sync.dma_start(out=k_words[:].bitcast(I32), in_=keys_words[0].bitcast(I32))
+        load_bytes(k_bytes, keys_scales)
+        nc.sync.dma_start(out=q_raw[:], in_=query.rearrange("(p j) w -> p j w", j=PACK))
+        nc.sync.dma_start(out=v_words[:].bitcast(I32), in_=vals_words[0].bitcast(I32))
+        load_bytes(v_bytes, vals_scales)
+        nc.sync.dma_start(out=g_raw[:], in_=gout.rearrange("(p j) w -> p j w", j=PACK))
+        nc.sync.dma_start(out=size_sb[:], in_=size.rearrange("o (p b) -> p (o b)", p=P))
+        nc.gpsimd.dma_start(out=steep_sb[:], in_=steep)
+        nc.gpsimd.dma_start(out=th_sb[:], in_=th)
+
+        def affine(dst, src, mul, add):
+            nc.scalar.activation(dst, src, ACT.Copy, bias=add, scale=mul)
+
+        ident = tile("ident", [P, P])
+        make_identity(nc, ident[:])
+
+        def quantise(name, raw):
+            grouped = tile(name + "_grouped", [P, Q, PACK], BF16)
+            codes = tile(name + "_codes", [P, Q], U32)
+            plane = tile(name + "_plane", [P, Q], U8)
+            nc.scalar.copy(grouped[:], raw[:].rearrange("p j w -> p w j"))
+            nc.vector.quantize_mx(
+                out=codes[:].bitcast(FP8X4), scales=plane[:], in_=grouped[:].rearrange("p w j -> p (w j)")
+            )
+            return codes, plane
+
+        def gather(name, window, dtype):
+            picked = tile(name, [P, I], dtype)
+            nc.vector.tensor_copy(picked[:], window[:].indirect(offsets[:]))
+            return picked
+
+        kw = gather("kw", k_words, U16)
+        kb = gather("kb", k_bytes, U8)
+        base_sb = tile("base_sb", [P, T], tag="pool_a")
+        nc.sync.dma_start(out=base_sb[:], in_=base)
+        q_codes, q_plane = quantise("q", q_raw)
+        a_ps = ps.tile([P, I], F32, name="a_ps")
+        nc.tensor.matmul_mx(
+            out=a_ps[:], lhsT=q_codes[:].bitcast(FP8X4), lhsT_scale=q_plane[:],
+            rhs=kw[:].bitcast(FP4X4), rhs_scale=kb[:], start=True, stop=True,
+        )
+        vb = gather("vb", v_bytes, U8)
+
+        row = tile("row", [P, 10], tag="raw_q")
+        neg_s16, s_th, pos_s16, neg_s4, pos_s4, s1, s1b, s1sq, neg_cb, factor = (row[:, n : n + 1] for n in range(10))
+        affine(neg_s16, steep_sb[:], -1.0 / 16, 0.0)
+        affine(s_th, steep_sb[:], th_sb[:], 0.0)
+        affine(pos_s16, steep_sb[:], 1.0 / 16, 0.0)
+        affine(neg_s4, steep_sb[:], -0.25, 0.0)
+        affine(pos_s4, steep_sb[:], 0.25, 0.0)
+        affine(s1, steep_sb[:], 0.25, 0.25)
+        affine(s1b, steep_sb[:], 0.1875, 0.1875)
+        affine(s1sq, s1, s1, 0.0)
+        affine(neg_cb, s1sq, -0.125, -0.0625)
+
+        nc.gpsimd.dma_start(out=gq1_sb[:], in_=gq1)
+        size_ps = ps.tile([P, I], F32, name="size_ps")
+        for b in range(I // P):
+            nc.tensor.transpose(size_ps[:, b * P : (b + 1) * P], size_sb[:, b : b + 1].to_broadcast([P, P]), ident[:])
+
+        a_sum = tile("a_sum", [P, G])
+        neg_max = tile("neg_max", [P, 1])
+        nc.vector.tensor_reduce(a_sum[:], paged(a_ps[:]), AX.X, ALU.add)
+        nc.vector.tensor_reduce(neg_max[:], a_ps[:], AX.X, ALU.max, negate=True)
+        g_codes, g_plane = quantise("g", g_raw)
+        closed = tile("closed", [P, G], tag="raw_g")
+        denom = tile("denom", [P, G])
+        r = tile("r", [P, I])
+        nc.scalar.activation(closed[:], a_sum[:], ACT.Exp, bias=s_th, scale=neg_s16)
+        nc.scalar.activation(denom[:], closed[:], ACT.Copy, bias=1.0)
+        nc.scalar.activation(r[:], a_ps[:], ACT.Exp, bias=neg_max[:])
+
+        vw = gather("vw", v_words, U16)
+        c_ps = ps.tile([P, I], F32, name="c_ps")
+        nc.tensor.matmul_mx(
+            out=c_ps[:], lhsT=g_codes[:].bitcast(FP8X4), lhsT_scale=g_plane[:],
+            rhs=vw[:].bitcast(FP4X4), rhs_scale=vb[:], start=True, stop=True,
+        )
+
+        gt = tile("gt", [P, G], tag="pool_v")
+        nc.vector.reciprocal(gt[:], denom[:])
+        p = tile("p", [P, I])
+        z = tile("z", [P, 1])
+        nc.vector.scalar_tensor_tensor(paged(p[:]), paged(r[:]), 1.0, spread(gt[:]), ALU.mult, ALU.mult, accum_out=z[:])
+        r_sum = tile("r_sum", [P, G])
+        nc.vector.tensor_reduce(r_sum[:], paged(r[:]), AX.X, ALU.add)
+        p_size = tile("p_size", [P, I])
+        nc.vector.tensor_tensor(
+            p_size[:].rearrange("p (n b) -> p n b", b=I // P),
+            size_ps[:].rearrange("p (b n) -> p n b", n=P),
+            p[:].rearrange("p (n b) -> p n b", b=I // P),
+            ALU.mult,
+        )
+        iz = tile("iz", [P, 1])
+        nc.vector.reciprocal(iz[:], z[:])
+
+        mixed = tile("mixed", [P, 5, G])
+        neg_j16 = mixed[:, 0, :]
+        coef = tile("coef", [P, 4, G])
+        sq_a = tile("sq_a", [P, G])
+        sq_b = tile("sq_b", [P, G])
+        b1 = tile("b1", [P, G])
+        a1h_sq = tile("a1h_sq", [P, G])
+        jb = tile("jb", [P, G])
+        nc.scalar.activation(sq_a[:], gt[:], ACT.Square, bias=s1, scale=neg_s4)
+        nc.scalar.activation(sq_b[:], gt[:], ACT.Square, bias=s1b, scale=neg_s4)
+        nc.scalar.activation(neg_j16, gt[:], ACT.Identity, bias=neg_s16, scale=pos_s16)
+        nc.scalar.activation(coef[:, 3, :], gt[:], ACT.Square, bias=pos_s4, scale=neg_s4)
+        nc.scalar.activation(b1[:], sq_b[:], ACT.Identity, bias=neg_cb, scale=2.0)
+        nc.scalar.activation(coef[:, 1, :], sq_a[:], ACT.Copy, bias=-0.03125, scale=0.5)
+        nc.scalar.activation(coef[:, 2, :], sq_a[:], ACT.Copy, bias=-0.0625)
+        nc.scalar.activation(a1h_sq[:], coef[:, 1, :], ACT.Square)
+        nc.gpsimd.tensor_tensor(jb[:], neg_j16, b1[:], ALU.mult)
+        nc.gpsimd.tensor_tensor(coef[:, 0, :], jb[:], a1h_sq[:], ALU.add)
+
+        affine(factor, gq1_sb[:], PENALTY, 0.0)
+        half_iz = tile("half_iz", [P, 1])
+        affine(half_iz[:], iz[:], 0.5, 0.0)
+        w = tile("w", [P, I])
+        nc.scalar.activation(w[:], p[:], ACT.Copy, scale=iz[:])
+        x = tile("x", [P, I])
+        zmu = tile("zmu", [P, 1])
+        nc.vector.scalar_tensor_tensor(x[:], c_ps[:], 1.0, p_size[:], ALU.mult, ALU.mult, accum_out=zmu[:])
+        py = tile("py", [P, 2, G])
+        p_sum, y_sum = py[:, 0, :], py[:, 1, :]
+        nc.vector.tensor_tensor(p_sum, r_sum[:], gt[:], ALU.mult)
+        x_sum = tile("x_sum", [P, G])
+        nc.vector.tensor_reduce(x_sum[:], paged(x[:]), AX.X, ALU.add)
+        neg_mu = tile("neg_mu", [P, 1])
+        nc.vector.tensor_scalar(neg_mu[:], zmu[:], iz[:], -1.0, ALU.mult, ALU.mult)
+        y = tile("y", [P, I])
+        nc.vector.scalar_tensor_tensor(y[:], p[:], neg_mu[:], x[:], ALU.mult, ALU.add)
+        nc.vector.scalar_tensor_tensor(y_sum, p_sum, neg_mu[:], x_sum[:], ALU.mult, ALU.add)
+
+        terms = tile("terms", [P, 4, G + 1])
+        y_sq = tile("y_sq", [P, I])
+        nc.scalar.activation(y_sq[:], y[:], ACT.Square, scale=iz[:], accum_out=terms[:, 3, G : G + 1])
+        wy = tile("wy", [P, I])
+        nc.vector.scalar_tensor_tensor(wy[:], y[:], half_iz[:], w[:], ALU.mult, ALU.mult, accum_out=terms[:, 2, G : G + 1])
+        nc.vector.scalar_tensor_tensor(
+            mixed[:, 1:5, :],
+            y_sum.unsqueeze(1).to_broadcast([P, 4, G]),
+            iz[:],
+            coef[:],
+            ALU.mult,
+            ALU.mult,
+        )
+        half_d, a1p = mixed[:, 2, :], mixed[:, 4, :]
+        y_sq_sum = tile("y_sq_sum", [P, G])
+        nc.vector.tensor_reduce(y_sq_sum[:], paged(y_sq[:]), AX.X, ALU.add)
+        nc.vector.scalar_tensor_tensor(
+            terms[:, :, 0:G].rearrange("p (a b) g -> p a b g", a=2),
+            py[:].unsqueeze(1).to_broadcast([P, 2, 2, G]),
+            iz[:],
+            mixed[:, 0:4, :].rearrange("p (a b) g -> p a b g", a=2),
+            ALU.mult,
+            ALU.mult,
+        )
+        u = tile("u", [P, I])
+        nc.vector.scalar_tensor_tensor(paged(u[:]), paged(y[:]), iz[:], spread(half_d), ALU.mult, ALU.add)
+        neg_ht = tile("neg_ht", [P, 2])
+        nc.vector.tensor_reduce(neg_ht[:], terms[:, 2:4, :], AX.X, ALU.add, negate=True)
+        neg_h2, neg_t = neg_ht[:, 0:1], neg_ht[:, 1:2]
+        sq = tile("sq", [P, I])
+        nc.scalar.activation(sq[:], u[:], ACT.Square, bias=neg_h2)
+
+        parts = tile("parts", [P, 3, G])
+        nc.vector.tensor_tensor(parts[:, 2, :], y_sq_sum[:], neg_j16, ALU.mult)
+        nc.vector.tensor_scalar(parts[:, 0, :], a1p, neg_h2, neg_h2, ALU.add, ALU.mult)
+        nc.vector.scalar_tensor_tensor(parts[:, 1, :], terms[:, 0, 0:G], neg_t, terms[:, 1, 0:G], ALU.mult, ALU.add)
+        neg_page = tile("neg_page", [P, G])
+        nc.vector.tensor_reduce(neg_page[:], parts[:].rearrange("p k g -> p g k"), AX.X, ALU.add)
+        v = tile("v", [P, I])
+        nc.vector.scalar_tensor_tensor(paged(v[:]), paged(w[:]), neg_t, spread(neg_page[:]), ALU.mult, ALU.subtract)
+        nc.vector.tensor_tensor(placed[:].indirect(offsets[:]), sq[:], v[:], ALU.add)
+
+        width = T // STORES
+        for n in range(STORES):
+            cols = slice(n * width, (n + 1) * width)
+            res = tile("res%d" % n, [P, width])
+            nc.vector.scalar_tensor_tensor(res[:], placed[:, cols], factor, base_sb[:, cols], ALU.mult, ALU.add)
+            nc.sync.dma_start(out=out[:, cols], in_=res[:])

@@ -7,9 +7,9 @@ D, E, T, I, Q, G = 512, 512, 2048, 512, 128, 32
 PAGE = I // G
 P = 128
 PACK = 4
-FLOPS = 2 * 2 * 512 * I * Q
+FLOPS = 2 * (D + E) * I * Q
 PENALTY = 512.0 * 2.0 * 512.0
-STORES = 4
+STORE_EDGES = (0, 256, 768, 1280, 1792, T)
 
 F32 = mybir.dt.float32
 BF16 = mybir.dt.bfloat16
@@ -42,21 +42,21 @@ def tile_attend_gppagegate_kernel(
             return ap.unsqueeze(2).to_broadcast([P, G, PAGE])
 
         offsets = sb.tile([P, I // 16], U16, name="offsets")
-        k_words = tile("k_words", [P, T], U16, tag="pool_a")
+        k_words = tile("k_words", [P, T], U16, tag="k_words_then_base")
+        v_words = tile("v_words", [P, T], U16, tag="v_words_then_sums")
         k_bytes = tile("k_bytes", [P, T], U8)
-        v_words = tile("v_words", [P, T], U16, tag="pool_v")
-        g_raw = tile("g_raw", [P, PACK, Q], tag="raw_g")
-        v_bytes = tile("v_bytes", [P, T], U8)
-        q_raw = tile("q_raw", [P, PACK, Q], tag="raw_q")
+        v_bytes = tile("v_bytes", [P, T], U8, tag="v_bytes_then_p")
+        q_raw = tile("q_raw", [P, PACK, Q], tag="query_then_rows")
+        g_raw = tile("g_raw", [P, PACK, Q])
         placed = tile("placed", [P, T])
         steep_sb = tile("steep_sb", [P, 1])
         th_sb = tile("th_sb", [P, 1])
         gq1_sb = tile("gq1_sb", [P, 1])
-        size_sb = tile("size_sb", [P, I // P])
+        size_sb = tile("size_sb", [P, PACK])
         warm = tile("warm", [P, 1])
         warm_out = tile("warm_out", [P, 1])
 
-        nc.vector.memset(k_bytes[:].bitcast(I32), 0)
+        nc.gpsimd.memset(k_bytes[:].bitcast(I32), 0)
         nc.vector.memset(v_bytes[:].bitcast(I32), 0)
         nc.vector.memset(warm[:], 0.0)
         nc.vector.memset(placed[:], 0.0)
@@ -70,21 +70,20 @@ def tile_attend_gppagegate_kernel(
                 )
 
         nc.sync.dma_start(offsets[:], offs)
-        nc.sync.dma_start(out=k_words[:].bitcast(I32), in_=keys_words[0].bitcast(I32))
-        load_bytes(k_bytes, keys_scales)
         nc.sync.dma_start(out=q_raw[:], in_=query.rearrange("(p j) w -> p j w", j=PACK))
+        nc.sync.dma_start(out=steep_sb[:], in_=steep)
+        load_bytes(k_bytes, keys_scales)
+        nc.sync.dma_start(out=k_words[:].bitcast(I32), in_=keys_words[0].bitcast(I32))
         nc.sync.dma_start(out=v_words[:].bitcast(I32), in_=vals_words[0].bitcast(I32))
-        load_bytes(v_bytes, vals_scales)
         nc.sync.dma_start(out=g_raw[:], in_=gout.rearrange("(p j) w -> p j w", j=PACK))
+        load_bytes(v_bytes, vals_scales)
         nc.sync.dma_start(out=size_sb[:], in_=size.rearrange("o (p b) -> p (o b)", p=P))
-        nc.gpsimd.dma_start(out=steep_sb[:], in_=steep)
         nc.gpsimd.dma_start(out=th_sb[:], in_=th)
-
-        def affine(dst, src, mul, add):
-            nc.scalar.activation(dst, src, ACT.Copy, bias=add, scale=mul)
-
         ident = tile("ident", [P, P])
         make_identity(nc, ident[:])
+        nc.gpsimd.dma_start(out=gq1_sb[:], in_=gq1)
+        factor = tile("factor", [P, 1])
+        nc.gpsimd.tensor_scalar(factor[:], gq1_sb[:], PENALTY, 0.0, ALU.mult, ALU.add)
 
         def quantise(name, raw):
             grouped = tile(name + "_grouped", [P, Q, PACK], BF16)
@@ -96,25 +95,38 @@ def tile_attend_gppagegate_kernel(
             )
             return codes, plane
 
-        def gather(name, window, dtype):
-            picked = tile(name, [P, I], dtype)
+        def gather(name, window, dtype, tag=None):
+            picked = tile(name, [P, I], dtype, tag=tag)
             nc.vector.tensor_copy(picked[:], window[:].indirect(offsets[:]))
             return picked
 
-        kw = gather("kw", k_words, U16)
+        def product(name, codes, plane, words, scale_bytes):
+            acc = ps.tile([P, I], F32, name=name)
+            nc.tensor.matmul_mx(
+                out=acc[:],
+                lhsT=codes[:].bitcast(FP8X4),
+                lhsT_scale=plane[:],
+                rhs=words[:].bitcast(FP4X4),
+                rhs_scale=scale_bytes[:],
+                start=True,
+                stop=True,
+            )
+            return acc
+
+        def affine(dst, src, mul, add):
+            nc.scalar.activation(dst, src, ACT.Copy, bias=add, scale=mul)
+
         kb = gather("kb", k_bytes, U8)
-        base_sb = tile("base_sb", [P, T], tag="pool_a")
+        kw = gather("kw", k_words, U16)
+        base_sb = tile("base_sb", [P, T], tag="k_words_then_base")
         nc.sync.dma_start(out=base_sb[:], in_=base)
         q_codes, q_plane = quantise("q", q_raw)
-        a_ps = ps.tile([P, I], F32, name="a_ps")
-        nc.tensor.matmul_mx(
-            out=a_ps[:], lhsT=q_codes[:].bitcast(FP8X4), lhsT_scale=q_plane[:],
-            rhs=kw[:].bitcast(FP4X4), rhs_scale=kb[:], start=True, stop=True,
-        )
-        vb = gather("vb", v_bytes, U8)
+        a_ps = product("a_ps", q_codes, q_plane, kw, kb)
+        vw = gather("vw", v_words, U16)
+        g_codes, g_plane = quantise("g", g_raw)
 
-        row = tile("row", [P, 10], tag="raw_q")
-        neg_s16, s_th, pos_s16, neg_s4, pos_s4, s1, s1b, s1sq, neg_cb, factor = (row[:, n : n + 1] for n in range(10))
+        row = tile("row", [P, 9], tag="query_then_rows")
+        neg_s16, s_th, pos_s16, neg_s4, pos_s4, s1, s1b, s1sq, neg_cb = (row[:, n : n + 1] for n in range(9))
         affine(neg_s16, steep_sb[:], -1.0 / 16, 0.0)
         affine(s_th, steep_sb[:], th_sb[:], 0.0)
         affine(pos_s16, steep_sb[:], 1.0 / 16, 0.0)
@@ -125,49 +137,43 @@ def tile_attend_gppagegate_kernel(
         affine(s1sq, s1, s1, 0.0)
         affine(neg_cb, s1sq, -0.125, -0.0625)
 
-        nc.gpsimd.dma_start(out=gq1_sb[:], in_=gq1)
-        size_ps = ps.tile([P, I], F32, name="size_ps")
-        for b in range(I // P):
-            nc.tensor.transpose(size_ps[:, b * P : (b + 1) * P], size_sb[:, b : b + 1].to_broadcast([P, P]), ident[:])
+        size_ps = ps.tile([P, PACK, P], F32, name="size_ps")
+        for b in range(PACK):
+            nc.tensor.transpose(size_ps[:, b, :], size_sb[:, b : b + 1].to_broadcast([P, P]), ident[:])
 
-        a_sum = tile("a_sum", [P, G])
+        a_sum = tile("a_sum", [P, G], tag="v_words_then_sums")
         neg_max = tile("neg_max", [P, 1])
         nc.vector.tensor_reduce(a_sum[:], paged(a_ps[:]), AX.X, ALU.add)
         nc.vector.tensor_reduce(neg_max[:], a_ps[:], AX.X, ALU.max, negate=True)
-        g_codes, g_plane = quantise("g", g_raw)
-        closed = tile("closed", [P, G], tag="raw_g")
+        closed = tile("closed", [P, G])
         denom = tile("denom", [P, G])
         r = tile("r", [P, I])
         nc.scalar.activation(closed[:], a_sum[:], ACT.Exp, bias=s_th, scale=neg_s16)
-        nc.scalar.activation(denom[:], closed[:], ACT.Copy, bias=1.0)
+        affine(denom[:], closed[:], 1.0, 1.0)
         nc.scalar.activation(r[:], a_ps[:], ACT.Exp, bias=neg_max[:])
 
-        vw = gather("vw", v_words, U16)
-        c_ps = ps.tile([P, I], F32, name="c_ps")
-        nc.tensor.matmul_mx(
-            out=c_ps[:], lhsT=g_codes[:].bitcast(FP8X4), lhsT_scale=g_plane[:],
-            rhs=vw[:].bitcast(FP4X4), rhs_scale=vb[:], start=True, stop=True,
-        )
+        vb = gather("vb", v_bytes, U8, tag="v_words_then_sums")
+        c_ps = product("c_ps", g_codes, g_plane, vw, vb)
 
-        gt = tile("gt", [P, G], tag="pool_v")
+        gt = tile("gt", [P, G])
         nc.vector.reciprocal(gt[:], denom[:])
-        p = tile("p", [P, I])
+        p_and_sum = tile("p_and_sum", [P, I + G], tag="v_bytes_then_p")
+        p, r_sum = p_and_sum[:, 0:I], p_and_sum[:, I : I + G]
         z = tile("z", [P, 1])
-        nc.vector.scalar_tensor_tensor(paged(p[:]), paged(r[:]), 1.0, spread(gt[:]), ALU.mult, ALU.mult, accum_out=z[:])
-        r_sum = tile("r_sum", [P, G])
-        nc.vector.tensor_reduce(r_sum[:], paged(r[:]), AX.X, ALU.add)
-        p_size = tile("p_size", [P, I])
-        nc.vector.tensor_tensor(
-            p_size[:].rearrange("p (n b) -> p n b", b=I // P),
-            size_ps[:].rearrange("p (b n) -> p n b", n=P),
-            p[:].rearrange("p (n b) -> p n b", b=I // P),
-            ALU.mult,
-        )
+        nc.vector.scalar_tensor_tensor(paged(p), paged(r[:]), 1.0, spread(gt[:]), ALU.mult, ALU.mult, accum_out=z[:])
+        nc.vector.tensor_reduce(r_sum, paged(r[:]), AX.X, ALU.add)
         iz = tile("iz", [P, 1])
         nc.vector.reciprocal(iz[:], z[:])
+        p_size = tile("p_size", [P, I])
+        nc.vector.tensor_tensor(
+            p_size[:].rearrange("p (n b) -> p n b", b=PACK),
+            size_ps[:].rearrange("p b n -> p n b"),
+            p.rearrange("p (n b) -> p n b", b=PACK),
+            ALU.mult,
+        )
 
         mixed = tile("mixed", [P, 5, G])
-        neg_j16 = mixed[:, 0, :]
+        j16 = mixed[:, 0, :]
         coef = tile("coef", [P, 4, G])
         sq_a = tile("sq_a", [P, G])
         sq_b = tile("sq_b", [P, G])
@@ -176,79 +182,65 @@ def tile_attend_gppagegate_kernel(
         jb = tile("jb", [P, G])
         nc.scalar.activation(sq_a[:], gt[:], ACT.Square, bias=s1, scale=neg_s4)
         nc.scalar.activation(sq_b[:], gt[:], ACT.Square, bias=s1b, scale=neg_s4)
-        nc.scalar.activation(neg_j16, gt[:], ACT.Identity, bias=neg_s16, scale=pos_s16)
+        nc.scalar.activation(j16, gt[:], ACT.Identity, bias=pos_s16, scale=neg_s16)
         nc.scalar.activation(coef[:, 3, :], gt[:], ACT.Square, bias=pos_s4, scale=neg_s4)
         nc.scalar.activation(b1[:], sq_b[:], ACT.Identity, bias=neg_cb, scale=2.0)
-        nc.scalar.activation(coef[:, 1, :], sq_a[:], ACT.Copy, bias=-0.03125, scale=0.5)
-        nc.scalar.activation(coef[:, 2, :], sq_a[:], ACT.Copy, bias=-0.0625)
+        affine(coef[:, 1, :], sq_a[:], -0.5, 0.03125)
+        affine(coef[:, 2, :], sq_a[:], 1.0, -0.0625)
         nc.scalar.activation(a1h_sq[:], coef[:, 1, :], ACT.Square)
-        nc.gpsimd.tensor_tensor(jb[:], neg_j16, b1[:], ALU.mult)
-        nc.gpsimd.tensor_tensor(coef[:, 0, :], jb[:], a1h_sq[:], ALU.add)
+        nc.gpsimd.tensor_tensor(jb[:], j16, b1[:], ALU.mult)
+        nc.gpsimd.tensor_tensor(coef[:, 0, :], jb[:], a1h_sq[:], ALU.subtract)
 
-        affine(factor, gq1_sb[:], PENALTY, 0.0)
-        half_iz = tile("half_iz", [P, 1])
-        affine(half_iz[:], iz[:], 0.5, 0.0)
         w = tile("w", [P, I])
-        nc.scalar.activation(w[:], p[:], ACT.Copy, scale=iz[:])
+        affine(w[:], p, iz[:], 0.0)
+        sums = tile("sums", [P, 2, G])
+        w_sum, neg_y_sum = sums[:, 0, :], sums[:, 1, :]
+        nc.vector.scalar_tensor_tensor(w_sum, r_sum, iz[:], gt[:], ALU.mult, ALU.mult)
         x = tile("x", [P, I])
-        zmu = tile("zmu", [P, 1])
-        nc.vector.scalar_tensor_tensor(x[:], c_ps[:], 1.0, p_size[:], ALU.mult, ALU.mult, accum_out=zmu[:])
-        py = tile("py", [P, 2, G])
-        p_sum, y_sum = py[:, 0, :], py[:, 1, :]
-        nc.vector.tensor_tensor(p_sum, r_sum[:], gt[:], ALU.mult)
+        mu = tile("mu", [P, 1])
+        nc.vector.scalar_tensor_tensor(x[:], c_ps[:], iz[:], p_size[:], ALU.mult, ALU.mult, accum_out=mu[:])
+        neg_y = tile("neg_y", [P, I])
+        nc.vector.scalar_tensor_tensor(neg_y[:], w[:], mu[:], x[:], ALU.mult, ALU.subtract)
         x_sum = tile("x_sum", [P, G])
         nc.vector.tensor_reduce(x_sum[:], paged(x[:]), AX.X, ALU.add)
-        neg_mu = tile("neg_mu", [P, 1])
-        nc.vector.tensor_scalar(neg_mu[:], zmu[:], iz[:], -1.0, ALU.mult, ALU.mult)
-        y = tile("y", [P, I])
-        nc.vector.scalar_tensor_tensor(y[:], p[:], neg_mu[:], x[:], ALU.mult, ALU.add)
-        nc.vector.scalar_tensor_tensor(y_sum, p_sum, neg_mu[:], x_sum[:], ALU.mult, ALU.add)
 
         terms = tile("terms", [P, 4, G + 1])
         y_sq = tile("y_sq", [P, I])
-        nc.scalar.activation(y_sq[:], y[:], ACT.Square, scale=iz[:], accum_out=terms[:, 3, G : G + 1])
+        nc.scalar.activation(y_sq[:], neg_y[:], ACT.Square, accum_out=terms[:, 3, G : G + 1])
         wy = tile("wy", [P, I])
-        nc.vector.scalar_tensor_tensor(wy[:], y[:], half_iz[:], w[:], ALU.mult, ALU.mult, accum_out=terms[:, 2, G : G + 1])
-        nc.vector.scalar_tensor_tensor(
-            mixed[:, 1:5, :],
-            y_sum.unsqueeze(1).to_broadcast([P, 4, G]),
-            iz[:],
-            coef[:],
-            ALU.mult,
-            ALU.mult,
-        )
-        half_d, a1p = mixed[:, 2, :], mixed[:, 4, :]
+        nc.vector.scalar_tensor_tensor(wy[:], neg_y[:], -0.5, w[:], ALU.mult, ALU.mult, accum_out=terms[:, 2, G : G + 1])
+        nc.vector.scalar_tensor_tensor(neg_y_sum, w_sum, mu[:], x_sum[:], ALU.mult, ALU.subtract)
         y_sq_sum = tile("y_sq_sum", [P, G])
         nc.vector.tensor_reduce(y_sq_sum[:], paged(y_sq[:]), AX.X, ALU.add)
-        nc.vector.scalar_tensor_tensor(
+        nc.vector.tensor_tensor(mixed[:, 1:5, :], coef[:], neg_y_sum.unsqueeze(1).to_broadcast([P, 4, G]), ALU.mult)
+        half_d, neg_jjy = mixed[:, 2, :], mixed[:, 4, :]
+        parts = tile("parts", [P, 3, G])
+        nc.vector.tensor_tensor(parts[:, 2, :], y_sq_sum[:], j16, ALU.mult)
+        nc.vector.tensor_tensor(
             terms[:, :, 0:G].rearrange("p (a b) g -> p a b g", a=2),
-            py[:].unsqueeze(1).to_broadcast([P, 2, 2, G]),
-            iz[:],
+            sums[:].unsqueeze(1).to_broadcast([P, 2, 2, G]),
             mixed[:, 0:4, :].rearrange("p (a b) g -> p a b g", a=2),
-            ALU.mult,
             ALU.mult,
         )
         u = tile("u", [P, I])
-        nc.vector.scalar_tensor_tensor(paged(u[:]), paged(y[:]), iz[:], spread(half_d), ALU.mult, ALU.add)
-        neg_ht = tile("neg_ht", [P, 2])
-        nc.vector.tensor_reduce(neg_ht[:], terms[:, 2:4, :], AX.X, ALU.add, negate=True)
-        neg_h2, neg_t = neg_ht[:, 0:1], neg_ht[:, 1:2]
+        nc.vector.tensor_tensor(paged(u[:]), spread(half_d), paged(neg_y[:]), ALU.subtract)
+        n_and_t = tile("n_and_t", [P, 2])
+        nc.vector.tensor_reduce(n_and_t[:], terms[:, 2:4, :], AX.X, ALU.add, negate=True)
+        n, neg_t = n_and_t[:, 0:1], n_and_t[:, 1:2]
         sq = tile("sq", [P, I])
-        nc.scalar.activation(sq[:], u[:], ACT.Square, bias=neg_h2)
+        nc.scalar.activation(sq[:], u[:], ACT.Square, bias=n)
 
-        parts = tile("parts", [P, 3, G])
-        nc.vector.tensor_tensor(parts[:, 2, :], y_sq_sum[:], neg_j16, ALU.mult)
-        nc.vector.tensor_scalar(parts[:, 0, :], a1p, neg_h2, neg_h2, ALU.add, ALU.mult)
+        nc.vector.tensor_scalar(parts[:, 0, :], neg_jjy, n, n, ALU.subtract, ALU.mult)
         nc.vector.scalar_tensor_tensor(parts[:, 1, :], terms[:, 0, 0:G], neg_t, terms[:, 1, 0:G], ALU.mult, ALU.add)
-        neg_page = tile("neg_page", [P, G])
-        nc.vector.tensor_reduce(neg_page[:], parts[:].rearrange("p k g -> p g k"), AX.X, ALU.add)
+        page_term = tile("page_term", [P, G])
+        nc.vector.tensor_reduce(page_term[:], parts[:].rearrange("p k g -> p g k"), AX.X, ALU.add)
         v = tile("v", [P, I])
-        nc.vector.scalar_tensor_tensor(paged(v[:]), paged(w[:]), neg_t, spread(neg_page[:]), ALU.mult, ALU.subtract)
+        nc.vector.scalar_tensor_tensor(paged(v[:]), paged(w[:]), neg_t, spread(page_term[:]), ALU.mult, ALU.add)
         nc.vector.tensor_tensor(placed[:].indirect(offsets[:]), sq[:], v[:], ALU.add)
 
-        width = T // STORES
-        for n in range(STORES):
-            cols = slice(n * width, (n + 1) * width)
-            res = tile("res%d" % n, [P, width])
-            nc.vector.scalar_tensor_tensor(res[:], placed[:, cols], factor, base_sb[:, cols], ALU.mult, ALU.add)
-            nc.sync.dma_start(out=out[:, cols], in_=res[:])
+        for first, last in zip(STORE_EDGES, STORE_EDGES[1:]):
+            res = tile("res%d" % first, [P, last - first])
+            nc.vector.scalar_tensor_tensor(
+                res[:], placed[:, first:last], factor[:], base_sb[:, first:last], ALU.mult, ALU.add
+            )
+            nc.sync.dma_start(out=out[:, first:last], in_=res[:])

@@ -56,7 +56,7 @@ def tile_attend_gppagegate_kernel(
         warm = tile("warm", [P, 1])
         warm_out = tile("warm_out", [P, 1])
 
-        nc.gpsimd.memset(k_bytes[:].bitcast(I32), 0)
+        nc.vector.memset(k_bytes[:].bitcast(I32), 0)
         nc.vector.memset(v_bytes[:].bitcast(I32), 0)
         nc.vector.memset(warm[:], 0.0)
         nc.vector.memset(placed[:], 0.0)
@@ -70,14 +70,14 @@ def tile_attend_gppagegate_kernel(
                 )
 
         nc.sync.dma_start(offsets[:], offs)
-        nc.sync.dma_start(out=q_raw[:], in_=query.rearrange("(p j) w -> p j w", j=PACK))
-        nc.sync.dma_start(out=steep_sb[:], in_=steep)
-        load_bytes(k_bytes, keys_scales)
         nc.sync.dma_start(out=k_words[:].bitcast(I32), in_=keys_words[0].bitcast(I32))
+        nc.sync.dma_start(out=q_raw[:], in_=query.rearrange("(p j) w -> p j w", j=PACK))
+        load_bytes(k_bytes, keys_scales)
         nc.sync.dma_start(out=v_words[:].bitcast(I32), in_=vals_words[0].bitcast(I32))
         nc.sync.dma_start(out=g_raw[:], in_=gout.rearrange("(p j) w -> p j w", j=PACK))
         load_bytes(v_bytes, vals_scales)
         nc.sync.dma_start(out=size_sb[:], in_=size.rearrange("o (p b) -> p (o b)", p=P))
+        nc.gpsimd.dma_start(out=steep_sb[:], in_=steep)
         nc.gpsimd.dma_start(out=th_sb[:], in_=th)
         ident = tile("ident", [P, P])
         make_identity(nc, ident[:])
@@ -116,8 +116,8 @@ def tile_attend_gppagegate_kernel(
         def affine(dst, src, mul, add):
             nc.scalar.activation(dst, src, ACT.Copy, bias=add, scale=mul)
 
-        kb = gather("kb", k_bytes, U8)
         kw = gather("kw", k_words, U16)
+        kb = gather("kb", k_bytes, U8)
         base_sb = tile("base_sb", [P, T], tag="k_words_then_base")
         nc.sync.dma_start(out=base_sb[:], in_=base)
         q_codes, q_plane = quantise("q", q_raw)
@@ -155,12 +155,11 @@ def tile_attend_gppagegate_kernel(
         vb = gather("vb", v_bytes, U8, tag="v_words_then_sums")
         c_ps = product("c_ps", g_codes, g_plane, vw, vb)
 
-        gt = tile("gt", [P, G])
-        nc.vector.reciprocal(gt[:], denom[:])
-        p_and_sum = tile("p_and_sum", [P, I + G], tag="v_bytes_then_p")
-        p, r_sum = p_and_sum[:, 0:I], p_and_sum[:, I : I + G]
+        gated = tile("gated", [P, I + 2 * G], tag="v_bytes_then_p")
+        p, r_sum, gt = gated[:, 0:I], gated[:, I : I + G], gated[:, I + G : I + 2 * G]
+        nc.vector.reciprocal(gt, denom[:])
         z = tile("z", [P, 1])
-        nc.vector.scalar_tensor_tensor(paged(p), paged(r[:]), 1.0, spread(gt[:]), ALU.mult, ALU.mult, accum_out=z[:])
+        nc.vector.scalar_tensor_tensor(paged(p), paged(r[:]), 1.0, spread(gt), ALU.mult, ALU.mult, accum_out=z[:])
         nc.vector.tensor_reduce(r_sum, paged(r[:]), AX.X, ALU.add)
         iz = tile("iz", [P, 1])
         nc.vector.reciprocal(iz[:], z[:])
@@ -180,10 +179,10 @@ def tile_attend_gppagegate_kernel(
         b1 = tile("b1", [P, G])
         a1h_sq = tile("a1h_sq", [P, G])
         jb = tile("jb", [P, G])
-        nc.scalar.activation(sq_a[:], gt[:], ACT.Square, bias=s1, scale=neg_s4)
-        nc.scalar.activation(sq_b[:], gt[:], ACT.Square, bias=s1b, scale=neg_s4)
-        nc.scalar.activation(j16, gt[:], ACT.Identity, bias=pos_s16, scale=neg_s16)
-        nc.scalar.activation(coef[:, 3, :], gt[:], ACT.Square, bias=pos_s4, scale=neg_s4)
+        nc.scalar.activation(sq_a[:], gt, ACT.Square, bias=s1, scale=neg_s4)
+        nc.scalar.activation(sq_b[:], gt, ACT.Square, bias=s1b, scale=neg_s4)
+        nc.scalar.activation(j16, gt, ACT.Identity, bias=pos_s16, scale=neg_s16)
+        nc.scalar.activation(coef[:, 3, :], gt, ACT.Square, bias=pos_s4, scale=neg_s4)
         nc.scalar.activation(b1[:], sq_b[:], ACT.Identity, bias=neg_cb, scale=2.0)
         affine(coef[:, 1, :], sq_a[:], -0.5, 0.03125)
         affine(coef[:, 2, :], sq_a[:], 1.0, -0.0625)
@@ -195,7 +194,7 @@ def tile_attend_gppagegate_kernel(
         affine(w[:], p, iz[:], 0.0)
         sums = tile("sums", [P, 2, G])
         w_sum, neg_y_sum = sums[:, 0, :], sums[:, 1, :]
-        nc.vector.scalar_tensor_tensor(w_sum, r_sum, iz[:], gt[:], ALU.mult, ALU.mult)
+        nc.vector.scalar_tensor_tensor(w_sum, r_sum, iz[:], gt, ALU.mult, ALU.mult)
         x = tile("x", [P, I])
         mu = tile("mu", [P, 1])
         nc.vector.scalar_tensor_tensor(x[:], c_ps[:], iz[:], p_size[:], ALU.mult, ALU.mult, accum_out=mu[:])

@@ -3,13 +3,14 @@ from contextlib import ExitStack
 import concourse.mybir as mybir
 from concourse.masks import make_identity
 
-D, E, T, I, Q, G = 512, 512, 2048, 512, 128, 32
-PAGE = I // G
+FEATURES, TOKENS, SLOTS, ROWS, PAGES = 512, 2048, 512, 128, 32
+PAGE = SLOTS // PAGES
 P = 128
 PACK = 4
-FLOPS = 2 * (D + E) * I * Q
+QUADRANT = 32
+FLOPS = 2 * 2 * FEATURES * SLOTS * ROWS
 PENALTY = 512.0 * 2.0 * 512.0
-STORE_EDGES = (0, 256, 768, 1280, 1792, T)
+STORE_EDGES = (0, 256, 768, 1280, 1792, TOKENS)
 
 F32 = mybir.dt.float32
 BF16 = mybir.dt.bfloat16
@@ -39,33 +40,29 @@ def tile_attend_gppagegate_kernel(
             return ap.rearrange("p (g s) -> p g s", s=PAGE)
 
         def spread(ap):
-            return ap.unsqueeze(2).to_broadcast([P, G, PAGE])
+            return ap.unsqueeze(2).to_broadcast([P, PAGES, PAGE])
 
-        offsets = sb.tile([P, I // 16], U16, name="offsets")
-        k_words = tile("k_words", [P, T], U16, tag="k_words_then_base")
-        v_words = tile("v_words", [P, T], U16, tag="v_words_then_sums")
-        k_bytes = tile("k_bytes", [P, T], U8)
-        v_bytes = tile("v_bytes", [P, T], U8, tag="v_bytes_then_p")
-        q_raw = tile("q_raw", [P, PACK, Q], tag="query_then_rows")
-        g_raw = tile("g_raw", [P, PACK, Q])
-        placed = tile("placed", [P, T])
+        offsets = sb.tile([P, SLOTS // 16], U16, name="offsets")
+        k_words = tile("k_words", [P, TOKENS], U16, tag="k_words_then_base")
+        v_words = tile("v_words", [P, TOKENS], U16, tag="v_words_then_sums")
+        k_bytes = tile("k_bytes", [P, TOKENS], U8)
+        v_bytes = tile("v_bytes", [P, TOKENS], U8, tag="v_bytes_then_gated")
+        q_raw = tile("q_raw", [P, PACK, ROWS], tag="query_then_rows")
+        g_raw = tile("g_raw", [P, PACK, ROWS])
+        placed = tile("placed", [P, TOKENS])
         steep_sb = tile("steep_sb", [P, 1])
         th_sb = tile("th_sb", [P, 1])
         gq1_sb = tile("gq1_sb", [P, 1])
         size_sb = tile("size_sb", [P, PACK])
-        warm = tile("warm", [P, 1])
-        warm_out = tile("warm_out", [P, 1])
 
         nc.vector.memset(k_bytes[:].bitcast(I32), 0)
         nc.vector.memset(v_bytes[:].bitcast(I32), 0)
-        nc.vector.memset(warm[:], 0.0)
         nc.vector.memset(placed[:], 0.0)
-        nc.scalar.activation(warm_out[:], warm[:], ACT.Exp)
 
         def load_bytes(plane, scales):
-            for quad in range(4):
+            for quad in range(P // QUADRANT):
                 nc.sync.dma_start(
-                    out=plane[32 * quad : 32 * quad + 4, :].bitcast(I32),
+                    out=plane[QUADRANT * quad : QUADRANT * quad + 4, :].bitcast(I32),
                     in_=scales[0, 4 * quad : 4 * quad + 4, :].bitcast(I32),
                 )
 
@@ -86,9 +83,9 @@ def tile_attend_gppagegate_kernel(
         nc.gpsimd.tensor_scalar(factor[:], gq1_sb[:], PENALTY, 0.0, ALU.mult, ALU.add)
 
         def quantise(name, raw):
-            grouped = tile(name + "_grouped", [P, Q, PACK], BF16)
-            codes = tile(name + "_codes", [P, Q], U32)
-            plane = tile(name + "_plane", [P, Q], U8)
+            grouped = tile(name + "_grouped", [P, ROWS, PACK], BF16)
+            codes = tile(name + "_codes", [P, ROWS], U32)
+            plane = tile(name + "_plane", [P, ROWS], U8)
             nc.scalar.copy(grouped[:], raw[:].rearrange("p j w -> p w j"))
             nc.vector.quantize_mx(
                 out=codes[:].bitcast(FP8X4), scales=plane[:], in_=grouped[:].rearrange("p w j -> p (w j)")
@@ -96,12 +93,12 @@ def tile_attend_gppagegate_kernel(
             return codes, plane
 
         def gather(name, window, dtype, tag=None):
-            picked = tile(name, [P, I], dtype, tag=tag)
+            picked = tile(name, [P, SLOTS], dtype, tag=tag)
             nc.vector.tensor_copy(picked[:], window[:].indirect(offsets[:]))
             return picked
 
         def product(name, codes, plane, words, scale_bytes):
-            acc = ps.tile([P, I], F32, name=name)
+            acc = ps.tile([P, SLOTS], F32, name=name)
             nc.tensor.matmul_mx(
                 out=acc[:],
                 lhsT=codes[:].bitcast(FP8X4),
@@ -118,7 +115,7 @@ def tile_attend_gppagegate_kernel(
 
         kw = gather("kw", k_words, U16)
         kb = gather("kb", k_bytes, U8)
-        base_sb = tile("base_sb", [P, T], tag="k_words_then_base")
+        base_sb = tile("base_sb", [P, TOKENS], tag="k_words_then_base")
         nc.sync.dma_start(out=base_sb[:], in_=base)
         q_codes, q_plane = quantise("q", q_raw)
         a_ps = product("a_ps", q_codes, q_plane, kw, kb)
@@ -126,7 +123,7 @@ def tile_attend_gppagegate_kernel(
         g_codes, g_plane = quantise("g", g_raw)
 
         row = tile("row", [P, 9], tag="query_then_rows")
-        neg_s16, s_th, pos_s16, neg_s4, pos_s4, s1, s1b, s1sq, neg_cb = (row[:, n : n + 1] for n in range(9))
+        neg_s16, s_th, pos_s16, neg_s4, pos_s4, s1, s1b, s1sq, neg_cb = (row[:, col : col + 1] for col in range(9))
         affine(neg_s16, steep_sb[:], -1.0 / 16, 0.0)
         affine(s_th, steep_sb[:], th_sb[:], 0.0)
         affine(pos_s16, steep_sb[:], 1.0 / 16, 0.0)
@@ -141,13 +138,13 @@ def tile_attend_gppagegate_kernel(
         for b in range(PACK):
             nc.tensor.transpose(size_ps[:, b, :], size_sb[:, b : b + 1].to_broadcast([P, P]), ident[:])
 
-        a_sum = tile("a_sum", [P, G], tag="v_words_then_sums")
+        a_sum = tile("a_sum", [P, PAGES], tag="v_words_then_sums")
         neg_max = tile("neg_max", [P, 1])
         nc.vector.tensor_reduce(a_sum[:], paged(a_ps[:]), AX.X, ALU.add)
         nc.vector.tensor_reduce(neg_max[:], a_ps[:], AX.X, ALU.max, negate=True)
-        closed = tile("closed", [P, G])
-        denom = tile("denom", [P, G])
-        r = tile("r", [P, I])
+        closed = tile("closed", [P, PAGES])
+        denom = tile("denom", [P, PAGES])
+        r = tile("r", [P, SLOTS])
         nc.scalar.activation(closed[:], a_sum[:], ACT.Exp, bias=s_th, scale=neg_s16)
         affine(denom[:], closed[:], 1.0, 1.0)
         nc.scalar.activation(r[:], a_ps[:], ACT.Exp, bias=neg_max[:])
@@ -155,15 +152,15 @@ def tile_attend_gppagegate_kernel(
         vb = gather("vb", v_bytes, U8, tag="v_words_then_sums")
         c_ps = product("c_ps", g_codes, g_plane, vw, vb)
 
-        gated = tile("gated", [P, I + 2 * G], tag="v_bytes_then_p")
-        p, r_sum, gt = gated[:, 0:I], gated[:, I : I + G], gated[:, I + G : I + 2 * G]
+        gated = tile("gated", [P, SLOTS + 2 * PAGES], tag="v_bytes_then_gated")
+        p, r_sum, gt = gated[:, 0:SLOTS], gated[:, SLOTS : SLOTS + PAGES], gated[:, SLOTS + PAGES : SLOTS + 2 * PAGES]
         nc.vector.reciprocal(gt, denom[:])
         z = tile("z", [P, 1])
         nc.vector.scalar_tensor_tensor(paged(p), paged(r[:]), 1.0, spread(gt), ALU.mult, ALU.mult, accum_out=z[:])
         nc.vector.tensor_reduce(r_sum, paged(r[:]), AX.X, ALU.add)
         iz = tile("iz", [P, 1])
         nc.vector.reciprocal(iz[:], z[:])
-        p_size = tile("p_size", [P, I])
+        p_size = tile("p_size", [P, SLOTS])
         nc.vector.tensor_tensor(
             p_size[:].rearrange("p (n b) -> p n b", b=PACK),
             size_ps[:].rearrange("p b n -> p n b"),
@@ -171,14 +168,14 @@ def tile_attend_gppagegate_kernel(
             ALU.mult,
         )
 
-        mixed = tile("mixed", [P, 5, G])
+        mixed = tile("mixed", [P, 5, PAGES])
         j16 = mixed[:, 0, :]
-        coef = tile("coef", [P, 4, G])
-        sq_a = tile("sq_a", [P, G])
-        sq_b = tile("sq_b", [P, G])
-        b1 = tile("b1", [P, G])
-        a1h_sq = tile("a1h_sq", [P, G])
-        jb = tile("jb", [P, G])
+        coef = tile("coef", [P, 4, PAGES])
+        sq_a = tile("sq_a", [P, PAGES])
+        sq_b = tile("sq_b", [P, PAGES])
+        b1 = tile("b1", [P, PAGES])
+        a1h_sq = tile("a1h_sq", [P, PAGES])
+        jb = tile("jb", [P, PAGES])
         nc.scalar.activation(sq_a[:], gt, ACT.Square, bias=s1, scale=neg_s4)
         nc.scalar.activation(sq_b[:], gt, ACT.Square, bias=s1b, scale=neg_s4)
         nc.scalar.activation(j16, gt, ACT.Identity, bias=pos_s16, scale=neg_s16)
@@ -190,53 +187,59 @@ def tile_attend_gppagegate_kernel(
         nc.gpsimd.tensor_tensor(jb[:], j16, b1[:], ALU.mult)
         nc.gpsimd.tensor_tensor(coef[:, 0, :], jb[:], a1h_sq[:], ALU.subtract)
 
-        w = tile("w", [P, I])
+        w = tile("w", [P, SLOTS])
         affine(w[:], p, iz[:], 0.0)
-        sums = tile("sums", [P, 2, G])
+        sums = tile("sums", [P, 2, PAGES])
         w_sum, neg_y_sum = sums[:, 0, :], sums[:, 1, :]
         nc.vector.scalar_tensor_tensor(w_sum, r_sum, iz[:], gt, ALU.mult, ALU.mult)
-        x = tile("x", [P, I])
+        x = tile("x", [P, SLOTS])
         mu = tile("mu", [P, 1])
         nc.vector.scalar_tensor_tensor(x[:], c_ps[:], iz[:], p_size[:], ALU.mult, ALU.mult, accum_out=mu[:])
-        neg_y = tile("neg_y", [P, I])
+        neg_y = tile("neg_y", [P, SLOTS])
         nc.vector.scalar_tensor_tensor(neg_y[:], w[:], mu[:], x[:], ALU.mult, ALU.subtract)
-        x_sum = tile("x_sum", [P, G])
+        x_sum = tile("x_sum", [P, PAGES])
         nc.vector.tensor_reduce(x_sum[:], paged(x[:]), AX.X, ALU.add)
 
-        terms = tile("terms", [P, 4, G + 1])
-        y_sq = tile("y_sq", [P, I])
-        nc.scalar.activation(y_sq[:], neg_y[:], ACT.Square, accum_out=terms[:, 3, G : G + 1])
-        wy = tile("wy", [P, I])
-        nc.vector.scalar_tensor_tensor(wy[:], neg_y[:], -0.5, w[:], ALU.mult, ALU.mult, accum_out=terms[:, 2, G : G + 1])
+        terms = tile("terms", [P, 4, PAGES + 1])
+        y_sq = tile("y_sq", [P, SLOTS])
+        nc.scalar.activation(y_sq[:], neg_y[:], ACT.Square, accum_out=terms[:, 3, PAGES : PAGES + 1])
+        wy = tile("wy", [P, SLOTS])
+        nc.vector.scalar_tensor_tensor(
+            wy[:], neg_y[:], -0.5, w[:], ALU.mult, ALU.mult, accum_out=terms[:, 2, PAGES : PAGES + 1]
+        )
         nc.vector.scalar_tensor_tensor(neg_y_sum, w_sum, mu[:], x_sum[:], ALU.mult, ALU.subtract)
-        y_sq_sum = tile("y_sq_sum", [P, G])
+        y_sq_sum = tile("y_sq_sum", [P, PAGES])
         nc.vector.tensor_reduce(y_sq_sum[:], paged(y_sq[:]), AX.X, ALU.add)
-        nc.vector.tensor_tensor(mixed[:, 1:5, :], coef[:], neg_y_sum.unsqueeze(1).to_broadcast([P, 4, G]), ALU.mult)
-        half_d, neg_jjy = mixed[:, 2, :], mixed[:, 4, :]
-        parts = tile("parts", [P, 3, G])
+        nc.vector.tensor_tensor(
+            mixed[:, 1:5, :], coef[:], neg_y_sum.unsqueeze(1).to_broadcast([P, 4, PAGES]), ALU.mult
+        )
+        half_dd, neg_jjy = mixed[:, 2, :], mixed[:, 4, :]
+        parts = tile("parts", [P, 3, PAGES])
         nc.vector.tensor_tensor(parts[:, 2, :], y_sq_sum[:], j16, ALU.mult)
         nc.vector.tensor_tensor(
-            terms[:, :, 0:G].rearrange("p (a b) g -> p a b g", a=2),
-            sums[:].unsqueeze(1).to_broadcast([P, 2, 2, G]),
+            terms[:, :, 0:PAGES].rearrange("p (a b) g -> p a b g", a=2),
+            sums[:].unsqueeze(1).to_broadcast([P, 2, 2, PAGES]),
             mixed[:, 0:4, :].rearrange("p (a b) g -> p a b g", a=2),
             ALU.mult,
         )
-        u = tile("u", [P, I])
-        nc.vector.tensor_tensor(paged(u[:]), spread(half_d), paged(neg_y[:]), ALU.subtract)
-        n_and_t = tile("n_and_t", [P, 2])
-        nc.vector.tensor_reduce(n_and_t[:], terms[:, 2:4, :], AX.X, ALU.add, negate=True)
-        n, neg_t = n_and_t[:, 0:1], n_and_t[:, 1:2]
-        sq = tile("sq", [P, I])
-        nc.scalar.activation(sq[:], u[:], ACT.Square, bias=n)
+        u = tile("u", [P, SLOTS])
+        nc.vector.tensor_tensor(paged(u[:]), spread(half_dd), paged(neg_y[:]), ALU.subtract)
+        shift_and_t = tile("shift_and_t", [P, 2])
+        nc.vector.tensor_reduce(shift_and_t[:], terms[:, 2:4, :], AX.X, ALU.add, negate=True)
+        shift, neg_t = shift_and_t[:, 0:1], shift_and_t[:, 1:2]
+        sq = tile("sq", [P, SLOTS])
+        nc.scalar.activation(sq[:], u[:], ACT.Square, bias=shift)
 
-        nc.vector.tensor_scalar(parts[:, 0, :], neg_jjy, n, n, ALU.subtract, ALU.mult)
-        nc.vector.scalar_tensor_tensor(parts[:, 1, :], terms[:, 0, 0:G], neg_t, terms[:, 1, 0:G], ALU.mult, ALU.add)
-        page_term = tile("page_term", [P, G])
+        nc.vector.tensor_scalar(parts[:, 0, :], neg_jjy, shift, shift, ALU.subtract, ALU.mult)
+        nc.vector.scalar_tensor_tensor(
+            parts[:, 1, :], terms[:, 0, 0:PAGES], neg_t, terms[:, 1, 0:PAGES], ALU.mult, ALU.add
+        )
+        page_term = tile("page_term", [P, PAGES])
         nc.vector.tensor_reduce(page_term[:], parts[:].rearrange("p k g -> p g k"), AX.X, ALU.add)
-        v = tile("v", [P, I])
-        nc.vector.scalar_tensor_tensor(paged(v[:]), paged(w[:]), neg_t, spread(page_term[:]), ALU.mult, ALU.add)
-        nc.vector.tensor_tensor(placed[:].indirect(offsets[:]), sq[:], v[:], ALU.add)
+        rest = tile("rest", [P, SLOTS])
+        nc.vector.scalar_tensor_tensor(paged(rest[:]), paged(w[:]), neg_t, spread(page_term[:]), ALU.mult, ALU.add)
 
+        nc.vector.tensor_tensor(placed[:].indirect(offsets[:]), sq[:], rest[:], ALU.add)
         for first, last in zip(STORE_EDGES, STORE_EDGES[1:]):
             res = tile("res%d" % first, [P, last - first])
             nc.vector.scalar_tensor_tensor(

from contextlib import ExitStack

import concourse.mybir as mybir
from concourse.masks import make_identity

FEATURES, TOKENS, SLOTS, ROWS, PAGES = 512, 2048, 512, 128, 32
PAGE = SLOTS // PAGES
P = 128
PACK = 4
QUADRANT = 32
FLOPS = 2 * 2 * FEATURES * SLOTS * ROWS
PENALTY = 512.0 * 2.0 * 512.0
STORE_EDGES = (0, 256, 768, 1280, 1792, TOKENS)

F32 = mybir.dt.float32
BF16 = mybir.dt.bfloat16
I32 = mybir.dt.int32
U32 = mybir.dt.uint32
U16 = mybir.dt.uint16
U8 = mybir.dt.uint8
FP8X4 = mybir.dt.float8_e4m3fn_x4
FP4X4 = mybir.dt.float4_e2m1fn_x4
ALU = mybir.AluOpType
ACT = mybir.ActivationFunctionType
AX = mybir.AxisListType


def tile_attend_gppagegate_kernel(
    tc, query, keys_words, keys_scales, th, steep, gout, vals_words, vals_scales, size, base, gq1, offs, out
):
    nc = tc.nc
    with ExitStack() as ctx:
        sb = ctx.enter_context(tc.tile_pool(name="sb", bufs=1))
        ps = ctx.enter_context(tc.psum_pool(name="ps", bufs=1))

        def tile(name, shape, dtype=F32, tag=None):
            return sb.tile(shape, dtype, name=name, tag=tag or name, align_bytes=64)

        def paged(ap):
            return ap.rearrange("p (g s) -> p g s", s=PAGE)

        def spread(ap):
            return ap.unsqueeze(2).to_broadcast([P, PAGES, PAGE])

        offsets = sb.tile([P, SLOTS // 16], U16, name="offsets")
        k_words = tile("k_words", [P, TOKENS], U16, tag="k_words_then_base")
        v_words = tile("v_words", [P, TOKENS], U16, tag="v_words_then_sums")
        k_bytes = tile("k_bytes", [P, TOKENS], U8)
        v_bytes = tile("v_bytes", [P, TOKENS], U8, tag="v_bytes_then_gated")
        q_raw = tile("q_raw", [P, PACK, ROWS], tag="query_then_rows")
        g_raw = tile("g_raw", [P, PACK, ROWS])
        placed = tile("placed", [P, TOKENS])
        steep_sb = tile("steep_sb", [P, 1])
        th_sb = tile("th_sb", [P, 1])
        gq1_sb = tile("gq1_sb", [P, 1])
        size_sb = tile("size_sb", [P, PACK])

        nc.vector.memset(k_bytes[:].bitcast(I32), 0)
        nc.vector.memset(v_bytes[:].bitcast(I32), 0)
        nc.vector.memset(placed[:], 0.0)

        def load_bytes(plane, scales):
            for quad in range(P // QUADRANT):
                nc.sync.dma_start(
                    out=plane[QUADRANT * quad : QUADRANT * quad + 4, :].bitcast(I32),
                    in_=scales[0, 4 * quad : 4 * quad + 4, :].bitcast(I32),
                )

        nc.sync.dma_start(offsets[:], offs)
        nc.sync.dma_start(out=k_words[:].bitcast(I32), in_=keys_words[0].bitcast(I32))
        nc.sync.dma_start(out=q_raw[:], in_=query.rearrange("(p j) w -> p j w", j=PACK))
        load_bytes(k_bytes, keys_scales)
        nc.sync.dma_start(out=v_words[:].bitcast(I32), in_=vals_words[0].bitcast(I32))
        nc.sync.dma_start(out=g_raw[:], in_=gout.rearrange("(p j) w -> p j w", j=PACK))
        load_bytes(v_bytes, vals_scales)
        nc.sync.dma_start(out=size_sb[:], in_=size.rearrange("o (p b) -> p (o b)", p=P))
        nc.gpsimd.dma_start(out=steep_sb[:], in_=steep)
        nc.gpsimd.dma_start(out=th_sb[:], in_=th)
        ident = tile("ident", [P, P])
        make_identity(nc, ident[:])
        nc.gpsimd.dma_start(out=gq1_sb[:], in_=gq1)
        factor = tile("factor", [P, 1])
        nc.gpsimd.tensor_scalar(factor[:], gq1_sb[:], PENALTY, 0.0, ALU.mult, ALU.add)

        def quantise(name, raw):
            grouped = tile(name + "_grouped", [P, ROWS, PACK], BF16)
            codes = tile(name + "_codes", [P, ROWS], U32)
            plane = tile(name + "_plane", [P, ROWS], U8)
            nc.scalar.copy(grouped[:], raw[:].rearrange("p j w -> p w j"))
            nc.vector.quantize_mx(
                out=codes[:].bitcast(FP8X4), scales=plane[:], in_=grouped[:].rearrange("p w j -> p (w j)")
            )
            return codes, plane

        def gather(name, window, dtype, tag=None):
            picked = tile(name, [P, SLOTS], dtype, tag=tag)
            nc.vector.tensor_copy(picked[:], window[:].indirect(offsets[:]))
            return picked

        def product(name, codes, plane, words, scale_bytes):
            acc = ps.tile([P, SLOTS], F32, name=name)
            nc.tensor.matmul_mx(
                out=acc[:],
                lhsT=codes[:].bitcast(FP8X4),
                lhsT_scale=plane[:],
                rhs=words[:].bitcast(FP4X4),
                rhs_scale=scale_bytes[:],
                start=True,
                stop=True,
            )
            return acc

        def affine(dst, src, mul, add):
            nc.scalar.activation(dst, src, ACT.Copy, bias=add, scale=mul)

        kw = gather("kw", k_words, U16)
        kb = gather("kb", k_bytes, U8)
        base_sb = tile("base_sb", [P, TOKENS], tag="k_words_then_base")
        nc.sync.dma_start(out=base_sb[:], in_=base)
        q_codes, q_plane = quantise("q", q_raw)
        a_ps = product("a_ps", q_codes, q_plane, kw, kb)
        vw = gather("vw", v_words, U16)
        g_codes, g_plane = quantise("g", g_raw)

        row = tile("row", [P, 9], tag="query_then_rows")
        neg_s16, s_th, pos_s16, neg_s4, pos_s4, s1, s1b, s1sq, neg_cb = (row[:, col : col + 1] for col in range(9))
        affine(neg_s16, steep_sb[:], -1.0 / 16, 0.0)
        affine(s_th, steep_sb[:], th_sb[:], 0.0)
        affine(pos_s16, steep_sb[:], 1.0 / 16, 0.0)
        affine(neg_s4, steep_sb[:], -0.25, 0.0)
        affine(pos_s4, steep_sb[:], 0.25, 0.0)
        affine(s1, steep_sb[:], 0.25, 0.25)
        affine(s1b, steep_sb[:], 0.1875, 0.1875)
        affine(s1sq, s1, s1, 0.0)
        affine(neg_cb, s1sq, -0.125, -0.0625)

        size_ps = ps.tile([P, PACK, P], F32, name="size_ps")
        for b in range(PACK):
            nc.tensor.transpose(size_ps[:, b, :], size_sb[:, b : b + 1].to_broadcast([P, P]), ident[:])

        a_sum = tile("a_sum", [P, PAGES], tag="v_words_then_sums")
        neg_max = tile("neg_max", [P, 1])
        nc.vector.tensor_reduce(a_sum[:], paged(a_ps[:]), AX.X, ALU.add)
        nc.vector.tensor_reduce(neg_max[:], a_ps[:], AX.X, ALU.max, negate=True)
        closed = tile("closed", [P, PAGES])
        denom = tile("denom", [P, PAGES])
        r = tile("r", [P, SLOTS])
        nc.scalar.activation(closed[:], a_sum[:], ACT.Exp, bias=s_th, scale=neg_s16)
        affine(denom[:], closed[:], 1.0, 1.0)
        nc.scalar.activation(r[:], a_ps[:], ACT.Exp, bias=neg_max[:])

        vb = gather("vb", v_bytes, U8, tag="v_words_then_sums")
        c_ps = product("c_ps", g_codes, g_plane, vw, vb)

        gated = tile("gated", [P, SLOTS + 2 * PAGES], tag="v_bytes_then_gated")
        p, r_sum, gt = gated[:, 0:SLOTS], gated[:, SLOTS : SLOTS + PAGES], gated[:, SLOTS + PAGES : SLOTS + 2 * PAGES]
        nc.vector.reciprocal(gt, denom[:])
        z = tile("z", [P, 1])
        nc.vector.scalar_tensor_tensor(paged(p), paged(r[:]), 1.0, spread(gt), ALU.mult, ALU.mult, accum_out=z[:])
        nc.vector.tensor_reduce(r_sum, paged(r[:]), AX.X, ALU.add)
        iz = tile("iz", [P, 1])
        nc.vector.reciprocal(iz[:], z[:])
        p_size = tile("p_size", [P, SLOTS])
        nc.vector.tensor_tensor(
            p_size[:].rearrange("p (n b) -> p n b", b=PACK),
            size_ps[:].rearrange("p b n -> p n b"),
            p.rearrange("p (n b) -> p n b", b=PACK),
            ALU.mult,
        )

        mixed = tile("mixed", [P, 5, PAGES])
        j16 = mixed[:, 0, :]
        coef = tile("coef", [P, 4, PAGES])
        sq_a = tile("sq_a", [P, PAGES])
        sq_b = tile("sq_b", [P, PAGES])
        b1 = tile("b1", [P, PAGES])
        a1h_sq = tile("a1h_sq", [P, PAGES])
        jb = tile("jb", [P, PAGES])
        nc.scalar.activation(sq_a[:], gt, ACT.Square, bias=s1, scale=neg_s4)
        nc.scalar.activation(sq_b[:], gt, ACT.Square, bias=s1b, scale=neg_s4)
        nc.scalar.activation(j16, gt, ACT.Identity, bias=pos_s16, scale=neg_s16)
        nc.scalar.activation(coef[:, 3, :], gt, ACT.Square, bias=pos_s4, scale=neg_s4)
        nc.scalar.activation(b1[:], sq_b[:], ACT.Identity, bias=neg_cb, scale=2.0)
        affine(coef[:, 1, :], sq_a[:], -0.5, 0.03125)
        affine(coef[:, 2, :], sq_a[:], 1.0, -0.0625)
        nc.scalar.activation(a1h_sq[:], coef[:, 1, :], ACT.Square)
        nc.gpsimd.tensor_tensor(jb[:], j16, b1[:], ALU.mult)
        nc.gpsimd.tensor_tensor(coef[:, 0, :], jb[:], a1h_sq[:], ALU.subtract)

        w = tile("w", [P, SLOTS])
        affine(w[:], p, iz[:], 0.0)
        sums = tile("sums", [P, 2, PAGES])
        w_sum, neg_y_sum = sums[:, 0, :], sums[:, 1, :]
        nc.vector.scalar_tensor_tensor(w_sum, r_sum, iz[:], gt, ALU.mult, ALU.mult)
        x = tile("x", [P, SLOTS])
        mu = tile("mu", [P, 1])
        nc.vector.scalar_tensor_tensor(x[:], c_ps[:], iz[:], p_size[:], ALU.mult, ALU.mult, accum_out=mu[:])
        neg_y = tile("neg_y", [P, SLOTS])
        nc.vector.scalar_tensor_tensor(neg_y[:], w[:], mu[:], x[:], ALU.mult, ALU.subtract)
        x_sum = tile("x_sum", [P, PAGES])
        nc.vector.tensor_reduce(x_sum[:], paged(x[:]), AX.X, ALU.add)

        terms = tile("terms", [P, 4, PAGES + 1])
        y_sq = tile("y_sq", [P, SLOTS])
        nc.scalar.activation(y_sq[:], neg_y[:], ACT.Square, accum_out=terms[:, 3, PAGES : PAGES + 1])
        wy = tile("wy", [P, SLOTS])
        nc.vector.scalar_tensor_tensor(
            wy[:], neg_y[:], -0.5, w[:], ALU.mult, ALU.mult, accum_out=terms[:, 2, PAGES : PAGES + 1]
        )
        nc.vector.scalar_tensor_tensor(neg_y_sum, w_sum, mu[:], x_sum[:], ALU.mult, ALU.subtract)
        y_sq_sum = tile("y_sq_sum", [P, PAGES])
        nc.vector.tensor_reduce(y_sq_sum[:], paged(y_sq[:]), AX.X, ALU.add)
        nc.vector.tensor_tensor(
            mixed[:, 1:5, :], coef[:], neg_y_sum.unsqueeze(1).to_broadcast([P, 4, PAGES]), ALU.mult
        )
        half_dd, neg_jjy = mixed[:, 2, :], mixed[:, 4, :]
        parts = tile("parts", [P, 3, PAGES])
        nc.vector.tensor_tensor(parts[:, 2, :], y_sq_sum[:], j16, ALU.mult)
        nc.vector.tensor_tensor(
            terms[:, :, 0:PAGES].rearrange("p (a b) g -> p a b g", a=2),
            sums[:].unsqueeze(1).to_broadcast([P, 2, 2, PAGES]),
            mixed[:, 0:4, :].rearrange("p (a b) g -> p a b g", a=2),
            ALU.mult,
        )
        u = tile("u", [P, SLOTS])
        nc.vector.tensor_tensor(paged(u[:]), spread(half_dd), paged(neg_y[:]), ALU.subtract)
        shift_and_t = tile("shift_and_t", [P, 2])
        nc.vector.tensor_reduce(shift_and_t[:], terms[:, 2:4, :], AX.X, ALU.add, negate=True)
        shift, neg_t = shift_and_t[:, 0:1], shift_and_t[:, 1:2]
        sq = tile("sq", [P, SLOTS])
        nc.scalar.activation(sq[:], u[:], ACT.Square, bias=shift)

        nc.vector.tensor_scalar(parts[:, 0, :], neg_jjy, shift, shift, ALU.subtract, ALU.mult)
        nc.vector.scalar_tensor_tensor(
            parts[:, 1, :], terms[:, 0, 0:PAGES], neg_t, terms[:, 1, 0:PAGES], ALU.mult, ALU.add
        )
        page_term = tile("page_term", [P, PAGES])
        nc.vector.tensor_reduce(page_term[:], parts[:].rearrange("p k g -> p g k"), AX.X, ALU.add)
        rest = tile("rest", [P, SLOTS])
        nc.vector.scalar_tensor_tensor(paged(rest[:]), paged(w[:]), neg_t, spread(page_term[:]), ALU.mult, ALU.add)

        nc.vector.tensor_tensor(placed[:].indirect(offsets[:]), sq[:], rest[:], ALU.add)
        for first, last in zip(STORE_EDGES, STORE_EDGES[1:]):
            res = tile("res%d" % first, [P, last - first])
            nc.vector.scalar_tensor_tensor(
                res[:], placed[:, first:last], factor[:], base_sb[:, first:last], ALU.mult, ALU.add
            )
            nc.sync.dma_start(out=out[:, first:last], in_=res[:])
